import numpy as np
import ml_dtypes


def mxq(x, axis, fmt="e4m3"):
    dtype, down = {"e4m3": (ml_dtypes.float8_e4m3fn, 7), "e5m2": (ml_dtypes.float8_e5m2, 14)}[fmt]
    v = np.moveaxis(np.asarray(x, np.float32).astype(ml_dtypes.bfloat16).astype(np.float64), axis, -1)
    blocks = v.reshape(v.shape[:-1] + (-1, 32))
    amax = np.abs(blocks).max(-1, keepdims=True)
    byte = np.maximum(np.where(amax > 0, np.frexp(amax)[1] - 1 + 127, 0) - down, 1)
    scale = np.exp2(byte - 127.0)
    codes = (blocks / scale).astype(np.float32).astype(dtype).astype(np.float64)
    return np.moveaxis((codes * scale).reshape(v.shape), -1, axis)


WIDE = False


def mx_kscale(k):
    if not WIDE:
        return np.ones(k)
    levels = np.array([30, -30])
    if k % 512:
        return np.exp2(np.random.permutation(np.resize(levels, k // 32))).repeat(32)
    a = np.empty((k // 512, 16))
    for p in range(k // 512):
        a[p, :8] = np.random.permutation(np.resize(levels, 8))
        for g in range(8):
            far = levels[np.abs(levels - a[p, g]) >= 10]
            a[p, g + 8] = far[np.random.randint(len(far))]
    return np.exp2(a.ravel()).repeat(32)


def f64(x):
    return np.asarray(x).astype(np.float64)


def striped(idx):
    return np.tile(np.asarray(idx).reshape(-1, 16).T, (8, 1)).astype(np.uint16)


def unstriped(offs):
    return offs[:16].T.reshape(-1).astype(np.int64)


E2M1 = np.array([0.0, 0.5, 1.0, 1.5, 2.0, 3.0, 4.0, 6.0, -0.0, -0.5, -1.0, -1.5, -2.0, -3.0, -4.0, -6.0])


def pack_weight(w, fmt):
    k, n = w.shape
    w = f64(np.asarray(w, np.float32).astype(ml_dtypes.bfloat16)).reshape(k // 32, 32, n)
    amax = np.abs(w).max(1)
    if fmt in ("e4m3", "e5m2"):
        byte = np.frexp(amax)[1] - 1 + 127 - (7 if fmt == "e4m3" else 14)
    else:
        mant, ex = np.frexp(amax / 6.0)
        byte = np.where(mant > 0.5, ex, ex - 1) + 127
    byte = np.clip(np.where(amax > 0, byte, 1), 1, 254)
    scaled = (w * np.exp2(127.0 - byte)[:, None, :]).reshape(k, n).astype(np.float32)
    by_word = np.ascontiguousarray(scaled.reshape(k // 512, 128, 4, n).transpose(0, 1, 3, 2))
    if fmt in ("e4m3", "e5m2"):
        words = by_word.astype(ml_dtypes.float8_e4m3fn if fmt == "e4m3" else ml_dtypes.float8_e5m2).view(np.uint8)
    else:
        c = by_word.astype(ml_dtypes.float4_e2m1fn).view(np.uint8) & 0xF
        words = (c[..., 0::2] | (c[..., 1::2] << 4)).reshape(k // 512, 128, 2 * n)
    return np.ascontiguousarray(words), np.ascontiguousarray(byte.astype(np.uint8).reshape(k // 512, 16, n))


def unpack_weight(words, scales, fmt):
    g, _, n = scales.shape
    words = np.ascontiguousarray(words).reshape(g, 128, n, -1)
    if fmt in ("e4m3", "e5m2"):
        vals = words.view(ml_dtypes.float8_e4m3fn if fmt == "e4m3" else ml_dtypes.float8_e5m2).astype(np.float64)
    else:
        nib = np.empty((g, 128, n, 4), np.uint8)
        nib[..., 0::2] = words & 0xF
        nib[..., 1::2] = words >> 4
        vals = E2M1[nib]
    vals = vals * np.repeat(np.exp2(scales.astype(np.float64) - 127.0), 8, axis=1)[..., None]
    return vals.transpose(0, 1, 3, 2).reshape(g * 512, n)


def sigmoid(v):
    return 1.0 / (1.0 + np.exp(-v))


K, F, T, Z, J, R, O, N, E = 512, 512, 1024, 1024, 256, 512, 128, 256, 512


def setup_inputs():
    n = np.random.standard_normal
    idx = np.random.permutation(T)[:J]
    idx2 = np.random.permutation(Z)[:J]
    idx3 = np.random.permutation(J)[:O]
    idx4 = np.random.permutation(J)[:O]
    idx5 = np.random.permutation(E)[:O]
    fk = mx_kscale(K)
    ff = mx_kscale(F)
    fr = mx_kscale(R)
    xtp = pack_weight(n((K, T)) / fk[:, None], "e5m2")
    wp = pack_weight(n((K, R)) * 1 / np.sqrt(K) * fk[:, None], "e2m1")
    xop = pack_weight(n((F, Z)) / ff[:, None], "e4m3")
    w2p = pack_weight(n((F, R)) * 1 / np.sqrt(F) * ff[:, None] * fr, "e2m1")
    wbp = pack_weight(n((R, N)) * 1 / np.sqrt(R) / fr[:, None], "e2m1")
    return {
        "xt_words": xtp[0],
        "xt_scales": xtp[1],
        "w_words": wp[0],
        "w_scales": wp[1],
        "xo_words": xop[0],
        "xo_scales": xop[1],
        "w2_words": w2p[0],
        "w2_scales": w2p[1],
        "sg": (np.random.uniform(0.6, 1.6, (R, 1))).astype(np.float32),
        "wb_words": wbp[0],
        "wb_scales": wbp[1],
        "tz": (n((N, E))).astype(np.float32),
        "so": (np.random.uniform(0.6, 1.6, (N, 1))).astype(np.float32),
        "bo": (np.random.uniform(-1.0, 1.0, (N, 1))).astype(np.float32),
        "offs": striped(idx),
        "offs2": striped(idx2),
        "offs3": striped(idx3),
        "offs4": striped(idx4),
        "offs5": striped(idx5),
    }


def reference(xt_words, xt_scales, w_words, w_scales, xo_words, xo_scales, w2_words, w2_scales, sg, wb_words, wb_scales, tz, so, bo, offs, offs2, offs3, offs4, offs5):
    idx = unstriped(offs)
    idx2 = unstriped(offs2)
    idx3 = unstriped(offs3)
    idx4 = unstriped(offs4)
    idx5 = unstriped(offs5)
    xtu = unpack_weight(xt_words, xt_scales, "e5m2")
    wu = unpack_weight(w_words, w_scales, "e2m1")
    xou = unpack_weight(xo_words, xo_scales, "e4m3")
    w2u = unpack_weight(w2_words, w2_scales, "e2m1")
    wbu = unpack_weight(wb_words, wb_scales, "e2m1")
    xtidxg = xtu[:, idx]
    a = wu.T @ xtidxg
    xoidx2g = xou[:, idx2]
    b = w2u.T @ xoidx2g
    hid = np.maximum(b[:, idx3], b[:, idx4]) * sigmoid(a[:, idx4] * f64(sg))
    hidq = mxq(hid, 0, "e4m3")
    p = wbu.T @ hidq
    y = p * sigmoid(f64(tz)[:, idx5] * f64(so) + f64(bo))
    return y

@@ -1,0 +1,176 @@
+from contextlib import ExitStack
+
+import concourse.mybir as mybir
+
+K, F, T, Z, J, R, O, N, E = 512, 512, 1024, 1024, 256, 512, 128, 256, 512
+FLOPS = 2 * K * R * J + 2 * F * R * J + 2 * R * N * O
+
+F32 = mybir.dt.float32
+BF16 = mybir.dt.bfloat16
+I32 = mybir.dt.int32
+U32 = mybir.dt.uint32
+U16 = mybir.dt.uint16
+U8 = mybir.dt.uint8
+E4M3 = mybir.dt.float8_e4m3fn_x4
+E5M2 = mybir.dt.float8_e5m2_x4
+E2M1 = mybir.dt.float4_e2m1fn_x4
+SIGMOID = mybir.ActivationFunctionType.Sigmoid
+COPY = mybir.ActivationFunctionType.Copy
+MULT = mybir.AluOpType.mult
+MAX = mybir.AluOpType.max
+
+P = 128
+PACK = 4
+QUADS = 4
+HALVES = N // P
+
+
+def load_scales(queue, plane, scales, quads):
+    for q in quads:
+        queue.dma_start(
+            out=plane[32 * q : 32 * q + 4, :].bitcast(I32),
+            in_=scales[0, 4 * q : 4 * q + 4, :].bitcast(I32),
+        )
+
+
+def tile_list_twotab_agree_one_finalgate_kernel(
+    tc, xt_words, xt_scales, w_words, w_scales, xo_words, xo_scales, w2_words, w2_scales,
+    sg, wb_words, wb_scales, tz, so, bo, offs, offs2, offs3, offs4, offs5, out,
+):
+    nc = tc.nc
+    with ExitStack() as ctx:
+        sb = ctx.enter_context(tc.tile_pool(name="sb", bufs=1))
+        ps = ctx.enter_context(tc.psum_pool(name="ps", bufs=1))
+
+        def tile(shape, dtype, name):
+            return sb.tile(shape, dtype, name=name, align_bytes=64)
+
+        list1 = tile([P, J // 16], U16, "list1")
+        list2 = tile([P, J // 16], U16, "list2")
+        list3 = tile([P, O // 16], U16, "list3")
+        list4 = tile([P, O // 16], U16, "list4")
+        list5 = tile([P, O // 16], U16, "list5")
+        xo_w = tile([P, Z], I32, "xo_w")
+        xt_w = tile([P, T], I32, "xt_w")
+        xo_s = tile([P, Z], U8, "xo_s")
+        xt_s = tile([P, T], U8, "xt_s")
+        w2_raw = tile([P, 2 * R], U8, "w2_raw")
+        w_raw = tile([P, 2 * R], U8, "w_raw")
+        w2_sraw = tile([P, R], U8, "w2_sraw")
+        w_sraw = tile([P, R], U8, "w_sraw")
+        wb_w = tile([P, 2 * N], U8, "wb_w")
+        wb_s = tile([P, N], U8, "wb_s")
+        sg_t = tile([P, PACK], F32, "sg_t")
+        so_t = tile([P, HALVES], F32, "so_t")
+        bo_t = tile([P, HALVES], F32, "bo_t")
+        tz_t = [tile([P, E], F32, "tz%d" % h) for h in range(HALVES)]
+
+        for plane in (xo_s, w2_sraw, xt_s, w_sraw, wb_s):
+            nc.vector.memset(plane[:].bitcast(I32), 0)
+
+        nc.gpsimd.dma_start(out=xo_w[:], in_=xo_words[0].rearrange("p n t -> p (n t)").bitcast(I32))
+        nc.gpsimd.dma_start(out=xt_w[:], in_=xt_words[0].rearrange("p n t -> p (n t)").bitcast(I32))
+        nc.sync.dma_start(list2[:], offs2)
+        load_scales(nc.sync, xo_s, xo_scales, range(QUADS))
+        nc.sync.dma_start(out=w2_raw[:].bitcast(I32), in_=w2_words[0].bitcast(I32))
+        nc.sync.dma_start(out=w_raw[:].bitcast(I32), in_=w_words[0].bitcast(I32))
+        load_scales(nc.sync, w2_sraw, w2_scales, range(QUADS))
+        nc.sync.dma_start(list1[:], offs)
+        load_scales(nc.sync, xt_s, xt_scales, range(QUADS))
+        load_scales(nc.gpsimd, w_sraw, w_scales, range(2))
+        load_scales(nc.sync, w_sraw, w_scales, range(2, QUADS))
+        nc.sync.dma_start(list3[:], offs3)
+        nc.sync.dma_start(list4[:], offs4)
+        nc.sync.dma_start(out=sg_t[:], in_=sg.rearrange("(p t) one -> p (t one)", t=PACK))
+        nc.sync.dma_start(list5[:], offs5)
+        for h in range(HALVES):
+            nc.sync.dma_start(out=tz_t[h][:], in_=tz[h * P : (h + 1) * P, :])
+        with nc.allow_non_contiguous_dma(reason="one value a partition and half"):
+            nc.sync.dma_start(out=so_t[:], in_=so.rearrange("(h p) one -> p (h one)", p=P))
+            nc.sync.dma_start(out=bo_t[:], in_=bo.rearrange("(h p) one -> p (h one)", p=P))
+        nc.sync.dma_start(out=wb_w[:].bitcast(I32), in_=wb_words[0].bitcast(I32))
+        load_scales(nc.sync, wb_s, wb_scales, range(QUADS))
+
+        def first_stage(name, words, plane, picks, fmt, raw, sraw, plane_tag):
+            wd = tile([P, 2 * R], U8, name + "_wd")
+            ws = tile([P, R], U8, name + "_ws")
+            gs = tile([P, J], U8, name + "_gs")
+            nc.scalar.copy(
+                out=wd[:].bitcast(U16).rearrange("p (t m) -> p t m", t=PACK),
+                in_=raw[:].bitcast(U16).rearrange("p (m t) -> p t m", t=PACK),
+            )
+            nc.vector.tensor_copy(out=gs[:], in_=plane[:].indirect(picks[:]))
+            gw = sb.tile([P, J], U32, name=name + "_gw", tag=plane_tag, align_bytes=64)
+            nc.vector.tensor_copy(out=gw[:], in_=words[:].bitcast(U32).indirect(picks[:]))
+            nc.vector.tensor_copy(
+                out=ws[:].rearrange("p (t m) -> p t m", t=PACK),
+                in_=sraw[:].rearrange("p (m t) -> p t m", t=PACK),
+            )
+            rows = []
+            for t in range(PACK):
+                acc = ps.tile([P, J], F32, name="%s_acc%d" % (name, t), tag="%s_bank%d" % (name, t))
+                nc.tensor.matmul_mx(
+                    out=acc[:],
+                    lhsT=wd[:, 2 * P * t : 2 * P * (t + 1)].bitcast(E2M1),
+                    lhsT_scale=ws[:, P * t : P * (t + 1)],
+                    rhs=gw[:].bitcast(fmt),
+                    rhs_scale=gs[:],
+                    start=True,
+                    stop=True,
+                )
+                row = tile([P, J], F32, "%s_row%d" % (name, t))
+                nc.scalar.copy(out=row[:], in_=acc[:])
+                rows.append(row)
+            return rows
+
+        b_rows = first_stage("b", xo_w, xo_s, list2, E4M3, w2_raw, w2_sraw, "xo_s")
+        a_rows = first_stage("a", xt_w, xt_s, list1, E5M2, w_raw, w_sraw, "xt_s")
+
+        b3 = tile([P, PACK, O], F32, "b3")
+        b4 = tile([P, PACK, O], F32, "b4")
+        sig = tile([P, PACK, O], F32, "sig")
+        top = tile([P, PACK, O], F32, "top")
+        for t in range(PACK):
+            nc.vector.tensor_copy(out=b3[:, t, :], in_=b_rows[t][:].indirect(list3[:]))
+            if t == 0:
+                nc.scalar.activation(out=b4[:, t, :], in_=b_rows[t][:].indirect(list4[:]), func=COPY)
+            else:
+                nc.vector.tensor_copy(out=b4[:, t, :], in_=b_rows[t][:].indirect(list4[:]))
+            nc.scalar.activation(
+                out=sig[:, t, :], in_=a_rows[t][:].indirect(list4[:]), func=SIGMOID,
+                scale=sg_t[:, t : t + 1],
+            )
+        gate = sb.tile([P, HALVES, O], F32, name="gate", tag="a_row3", align_bytes=64)
+        for h in range(HALVES):
+            nc.scalar.activation(
+                out=gate[:, h, :], in_=tz_t[h][:].indirect(list5[:]), func=SIGMOID,
+                bias=bo_t[:, h : h + 1], scale=so_t[:, h : h + 1],
+            )
+
+        nc.vector.tensor_tensor(out=top[:], in0=b3[:], in1=b4[:], op=MAX)
+        hid = tile([P, O, PACK], BF16, "hid")
+        nc.vector.tensor_tensor(
+            out=hid[:].rearrange("p (c i) t -> p c t i", i=4),
+            in0=top[:].rearrange("p t (c i) -> p c t i", i=4),
+            in1=sig[:].rearrange("p t (c i) -> p c t i", i=4),
+            op=MULT,
+        )
+        hid_w = tile([P, O], U32, "hid_w")
+        hid_s = tile([P, O], U8, "hid_s")
+        nc.vector.quantize_mx(
+            out=hid_w[:].bitcast(E4M3), scales=hid_s[:], in_=hid[:].rearrange("p o t -> p (o t)")
+        )
+        for h, queue in enumerate((nc.sync, nc.scalar)):
+            pacc = ps.tile([P, O], F32, name="pacc%d" % h, tag="b_bank%d" % h)
+            nc.tensor.matmul_mx(
+                out=pacc[:],
+                lhsT=wb_w[:, 2 * P * h : 2 * P * (h + 1)].bitcast(E2M1),
+                lhsT_scale=wb_s[:, P * h : P * (h + 1)],
+                rhs=hid_w[:].bitcast(E4M3),
+                rhs_scale=hid_s[:],
+                start=True,
+                stop=True,
+            )
+            res = tile([P, O], F32, "res%d" % h)
+            nc.vector.tensor_tensor(out=res[:], in0=pacc[:], in1=gate[:, h, :], op=MULT)
+            queue.dma_start(out=out[h * P : (h + 1) * P, :], in_=res[:])

@@ -68,6 +68,9 @@ def tile_list_twotab_agree_one_finalgate_kernel(
         for plane in (xo_s, w2_sraw, xt_s, w_sraw, wb_s):
             nc.vector.memset(plane[:].bitcast(I32), 0)
 
+        warm = tile([P, 2], F32, "warm")
+        nc.vector.memset(warm[:, 0:1], 0.0)
+        nc.scalar.activation(out=warm[:, 1:2], in_=warm[:, 0:1], func=SIGMOID)
         nc.gpsimd.dma_start(out=xo_w[:], in_=xo_words[0].rearrange("p n t -> p (n t)").bitcast(I32))
         nc.gpsimd.dma_start(out=xt_w[:], in_=xt_words[0].rearrange("p n t -> p (n t)").bitcast(I32))
         nc.sync.dma_start(list2[:], offs2)

@@ -65,34 +65,37 @@ def tile_list_twotab_agree_one_finalgate_kernel(
         bo_t = tile([P, HALVES], F32, "bo_t")
         tz_t = [tile([P, E], F32, "tz%d" % h) for h in range(HALVES)]
 
-        for plane in (xo_s, w2_sraw, xt_s, w_sraw, wb_s):
-            nc.vector.memset(plane[:].bitcast(I32), 0)
+        nc.vector.memset(xo_s[:].bitcast(I32), 0)
+        for plane in (w2_sraw, xt_s, w_sraw, wb_s):
+            words = plane[:].bitcast(I32)
+            cut = words.shape[1] // 2 + 1
+            nc.vector.memset(words[:, :cut], 0)
+            nc.vector.memset(words[:, cut:], 0)
 
+        nc.scalar.dma_start(out=w2_raw[:].bitcast(I32), in_=w2_words[0].bitcast(I32))
+        nc.scalar.dma_start(out=w_raw[:].bitcast(I32), in_=w_words[0].bitcast(I32))
         warm = tile([P, 2], F32, "warm")
         nc.vector.memset(warm[:, 0:1], 0.0)
         nc.scalar.activation(out=warm[:, 1:2], in_=warm[:, 0:1], func=SIGMOID)
-        nc.gpsimd.dma_start(out=xo_w[:], in_=xo_words[0].rearrange("p n t -> p (n t)").bitcast(I32))
+        nc.gpsimd.dma_start(out=sg_t[:], in_=sg.rearrange("(p t) one -> p (t one)", t=PACK))
         nc.gpsimd.dma_start(out=xt_w[:], in_=xt_words[0].rearrange("p n t -> p (n t)").bitcast(I32))
+        nc.gpsimd.dma_start(out=wb_w[:].bitcast(I32), in_=wb_words[0].bitcast(I32))
         nc.sync.dma_start(list2[:], offs2)
         load_scales(nc.sync, xo_s, xo_scales, range(QUADS))
-        nc.sync.dma_start(out=w2_raw[:].bitcast(I32), in_=w2_words[0].bitcast(I32))
-        nc.sync.dma_start(out=w_raw[:].bitcast(I32), in_=w_words[0].bitcast(I32))
+        nc.sync.dma_start(out=xo_w[:], in_=xo_words[0].rearrange("p n t -> p (n t)").bitcast(I32))
         load_scales(nc.sync, w2_sraw, w2_scales, range(QUADS))
         nc.sync.dma_start(list1[:], offs)
         load_scales(nc.sync, xt_s, xt_scales, range(QUADS))
-        load_scales(nc.gpsimd, w_sraw, w_scales, range(2))
-        load_scales(nc.sync, w_sraw, w_scales, range(2, QUADS))
-        nc.sync.dma_start(list3[:], offs3)
+        load_scales(nc.sync, w_sraw, w_scales, range(QUADS))
         nc.sync.dma_start(list4[:], offs4)
-        nc.sync.dma_start(out=sg_t[:], in_=sg.rearrange("(p t) one -> p (t one)", t=PACK))
+        nc.sync.dma_start(list3[:], offs3)
+        load_scales(nc.sync, wb_s, wb_scales, range(QUADS))
         nc.sync.dma_start(list5[:], offs5)
+        with nc.allow_non_contiguous_dma(reason="one value a partition and half"):
+            nc.gpsimd.dma_start(out=so_t[:], in_=so.rearrange("(h p) one -> p (h one)", p=P))
+            nc.sync.dma_start(out=bo_t[:], in_=bo.rearrange("(h p) one -> p (h one)", p=P))
         for h in range(HALVES):
             nc.sync.dma_start(out=tz_t[h][:], in_=tz[h * P : (h + 1) * P, :])
-        with nc.allow_non_contiguous_dma(reason="one value a partition and half"):
-            nc.sync.dma_start(out=so_t[:], in_=so.rearrange("(h p) one -> p (h one)", p=P))
-            nc.sync.dma_start(out=bo_t[:], in_=bo.rearrange("(h p) one -> p (h one)", p=P))
-        nc.sync.dma_start(out=wb_w[:].bitcast(I32), in_=wb_words[0].bitcast(I32))
-        load_scales(nc.sync, wb_s, wb_scales, range(QUADS))
 
         def first_stage(name, words, plane, picks, fmt, raw, sraw, plane_tag):
             wd = tile([P, 2 * R], U8, name + "_wd")
@@ -127,18 +130,19 @@ def tile_list_twotab_agree_one_finalgate_kernel(
             return rows
 
         b_rows = first_stage("b", xo_w, xo_s, list2, E4M3, w2_raw, w2_sraw, "xo_s")
-        a_rows = first_stage("a", xt_w, xt_s, list1, E5M2, w_raw, w_sraw, "xt_s")
+        a_rows = first_stage("a", xt_w, xt_s, list1, E5M2, w_raw, w_sraw, "a_gw")
 
         b3 = tile([P, PACK, O], F32, "b3")
         b4 = tile([P, PACK, O], F32, "b4")
         sig = tile([P, PACK, O], F32, "sig")
         top = tile([P, PACK, O], F32, "top")
         for t in range(PACK):
-            nc.vector.tensor_copy(out=b3[:, t, :], in_=b_rows[t][:].indirect(list3[:]))
-            if t == 0:
+            if t < 2:
                 nc.scalar.activation(out=b4[:, t, :], in_=b_rows[t][:].indirect(list4[:]), func=COPY)
             else:
                 nc.vector.tensor_copy(out=b4[:, t, :], in_=b_rows[t][:].indirect(list4[:]))
+        for t in range(PACK):
+            nc.vector.tensor_copy(out=b3[:, t, :], in_=b_rows[t][:].indirect(list3[:]))
             nc.scalar.activation(
                 out=sig[:, t, :], in_=a_rows[t][:].indirect(list4[:]), func=SIGMOID,
                 scale=sg_t[:, t : t + 1],

@@ -42,8 +42,8 @@ def tile_list_twotab_agree_one_finalgate_kernel(
         sb = ctx.enter_context(tc.tile_pool(name="sb", bufs=1))
         ps = ctx.enter_context(tc.psum_pool(name="ps", bufs=1))
 
-        def tile(shape, dtype, name):
-            return sb.tile(shape, dtype, name=name, align_bytes=64)
+        def tile(shape, dtype, name, tag=None):
+            return sb.tile(shape, dtype, name=name, tag=tag or name, align_bytes=64)
 
         list1 = tile([P, J // 16], U16, "list1")
         list2 = tile([P, J // 16], U16, "list2")
@@ -65,54 +65,79 @@ def tile_list_twotab_agree_one_finalgate_kernel(
         bo_t = tile([P, HALVES], F32, "bo_t")
         tz_t = [tile([P, E], F32, "tz%d" % h) for h in range(HALVES)]
 
-        nc.vector.memset(xo_s[:].bitcast(I32), 0)
-        for plane in (w2_sraw, xt_s, w_sraw, wb_s):
+        def clear_odd(plane):
             words = plane[:].bitcast(I32)
             cut = words.shape[1] // 2 + 1
             nc.vector.memset(words[:, :cut], 0)
             nc.vector.memset(words[:, cut:], 0)
 
-        nc.scalar.dma_start(out=w2_raw[:].bitcast(I32), in_=w2_words[0].bitcast(I32))
-        nc.scalar.dma_start(out=w_raw[:].bitcast(I32), in_=w_words[0].bitcast(I32))
-        warm = tile([P, 2], F32, "warm")
-        nc.vector.memset(warm[:, 0:1], 0.0)
-        nc.scalar.activation(out=warm[:, 1:2], in_=warm[:, 0:1], func=SIGMOID)
-        nc.gpsimd.dma_start(out=sg_t[:], in_=sg.rearrange("(p t) one -> p (t one)", t=PACK))
-        nc.gpsimd.dma_start(out=xt_w[:], in_=xt_words[0].rearrange("p n t -> p (n t)").bitcast(I32))
-        nc.gpsimd.dma_start(out=wb_w[:].bitcast(I32), in_=wb_words[0].bitcast(I32))
+        def load_table(queue, dst, words):
+            queue.dma_start(out=dst[:], in_=words[0].rearrange("p n t -> p (n t)").bitcast(I32))
+
+        def load_raw(queue, dst, words):
+            queue.dma_start(out=dst[:].bitcast(I32), in_=words[0].bitcast(I32))
+
+        def load_cols(queue, dst, vec):
+            with nc.allow_non_contiguous_dma(reason="one value a partition and half"):
+                queue.dma_start(out=dst[:], in_=vec.rearrange("(h p) one -> p (h one)", p=P))
+
+        def load_sg(queue):
+            queue.dma_start(out=sg_t[:], in_=sg.rearrange("(p t) one -> p (t one)", t=PACK))
+
+        def load_tz(queue, h):
+            queue.dma_start(out=tz_t[h][:], in_=tz[h * P : (h + 1) * P, :])
+
+        def warm_up():
+            warm = tile([P, 2], F32, "warm")
+            nc.vector.memset(warm[:, 0:1], 0.0)
+            nc.scalar.activation(out=warm[:, 1:2], in_=warm[:, 0:1], func=SIGMOID)
+
+        nc.vector.memset(w2_sraw[:].bitcast(I32), 0)
+        nc.vector.memset(w_sraw[:].bitcast(I32), 0)
+        for plane in (xo_s, xt_s, wb_s):
+            clear_odd(plane)
+        load_scales(nc.gpsimd, w_sraw, w_scales, range(2, 4))
+        load_scales(nc.gpsimd, wb_s, wb_scales, range(QUADS))
+        load_raw(nc.scalar, w2_raw, w2_words)
+        load_scales(nc.scalar, w2_sraw, w2_scales, range(2, 4))
+        load_table(nc.scalar, xo_w, xo_words)
+        warm_up()
         nc.sync.dma_start(list2[:], offs2)
+        load_raw(nc.sync, w_raw, w_words)
+        load_scales(nc.sync, w2_sraw, w2_scales, range(2))
         load_scales(nc.sync, xo_s, xo_scales, range(QUADS))
-        nc.sync.dma_start(out=xo_w[:], in_=xo_words[0].rearrange("p n t -> p (n t)").bitcast(I32))
-        load_scales(nc.sync, w2_sraw, w2_scales, range(QUADS))
+        load_scales(nc.sync, w_sraw, w_scales, range(2))
+        load_table(nc.sync, xt_w, xt_words)
         nc.sync.dma_start(list1[:], offs)
         load_scales(nc.sync, xt_s, xt_scales, range(QUADS))
-        load_scales(nc.sync, w_sraw, w_scales, range(QUADS))
         nc.sync.dma_start(list4[:], offs4)
         nc.sync.dma_start(list3[:], offs3)
-        load_scales(nc.sync, wb_s, wb_scales, range(QUADS))
+        load_sg(nc.sync)
         nc.sync.dma_start(list5[:], offs5)
-        with nc.allow_non_contiguous_dma(reason="one value a partition and half"):
-            nc.gpsimd.dma_start(out=so_t[:], in_=so.rearrange("(h p) one -> p (h one)", p=P))
-            nc.sync.dma_start(out=bo_t[:], in_=bo.rearrange("(h p) one -> p (h one)", p=P))
-        for h in range(HALVES):
-            nc.sync.dma_start(out=tz_t[h][:], in_=tz[h * P : (h + 1) * P, :])
+        load_cols(nc.sync, so_t, so)
+        load_cols(nc.sync, bo_t, bo)
+        load_tz(nc.sync, 0)
+        load_tz(nc.sync, 1)
+        load_raw(nc.sync, wb_w, wb_words)
 
-        def first_stage(name, words, plane, picks, fmt, raw, sraw, plane_tag):
-            wd = tile([P, 2 * R], U8, name + "_wd")
-            ws = tile([P, R], U8, name + "_ws")
-            gs = tile([P, J], U8, name + "_gs")
+        def deal_words(name, raw):
+            wd = tile([P, 2 * R], U8, name)
             nc.scalar.copy(
                 out=wd[:].bitcast(U16).rearrange("p (t m) -> p t m", t=PACK),
                 in_=raw[:].bitcast(U16).rearrange("p (m t) -> p t m", t=PACK),
             )
-            nc.vector.tensor_copy(out=gs[:], in_=plane[:].indirect(picks[:]))
-            gw = sb.tile([P, J], U32, name=name + "_gw", tag=plane_tag, align_bytes=64)
-            nc.vector.tensor_copy(out=gw[:], in_=words[:].bitcast(U32).indirect(picks[:]))
+            return wd
+
+        def deal_scales(name, sraw):
+            ws = tile([P, R], U8, name)
             nc.vector.tensor_copy(
                 out=ws[:].rearrange("p (t m) -> p t m", t=PACK),
                 in_=sraw[:].rearrange("p (m t) -> p t m", t=PACK),
             )
-            rows = []
+            return ws
+
+        def products(name, wd, ws, gw, gs, fmt):
+            accs = []
             for t in range(PACK):
                 acc = ps.tile([P, J], F32, name="%s_acc%d" % (name, t), tag="%s_bank%d" % (name, t))
                 nc.tensor.matmul_mx(
@@ -124,36 +149,57 @@ def tile_list_twotab_agree_one_finalgate_kernel(
                     start=True,
                     stop=True,
                 )
-                row = tile([P, J], F32, "%s_row%d" % (name, t))
-                nc.scalar.copy(out=row[:], in_=acc[:])
-                rows.append(row)
-            return rows
+                accs.append(acc)
+            return accs
 
-        b_rows = first_stage("b", xo_w, xo_s, list2, E4M3, w2_raw, w2_sraw, "xo_s")
-        a_rows = first_stage("a", xt_w, xt_s, list1, E5M2, w_raw, w_sraw, "a_gw")
+        w2_d = deal_words("w2_d", w2_raw)
+        w_d = deal_words("w_d", w_raw)
+
+        w2_ds = deal_scales("w2_ds", w2_sraw)
+        xo_gw = tile([P, J], U32, "xo_gw")
+        xo_gs = tile([P, J], U8, "xo_gs")
+        nc.vector.tensor_copy(out=xo_gw[:], in_=xo_w[:].bitcast(U32).indirect(list2[:]))
+        nc.vector.tensor_copy(out=xo_gs[:], in_=xo_s[:].indirect(list2[:]))
+        b_acc = products("b", w2_d, w2_ds, xo_gw, xo_gs, E4M3)
+        b_rows = [tile([P, J], F32, "b_row%d" % t) for t in range(PACK)]
+        for t in range(PACK):
+            nc.scalar.copy(out=b_rows[t][:], in_=b_acc[t][:])
+
+        w_ds = deal_scales("w_ds", w_sraw)
+        xt_gw = tile([P, J], U32, "xt_gw", tag="w_sraw")
+        xt_gs = tile([P, J], U8, "xt_gs")
+        nc.vector.tensor_copy(out=xt_gw[:], in_=xt_w[:].bitcast(U32).indirect(list1[:]))
+        nc.vector.tensor_copy(out=xt_gs[:], in_=xt_s[:].indirect(list1[:]))
+        a_acc = products("a", w_d, w_ds, xt_gw, xt_gs, E5M2)
 
         b3 = tile([P, PACK, O], F32, "b3")
         b4 = tile([P, PACK, O], F32, "b4")
         sig = tile([P, PACK, O], F32, "sig")
         top = tile([P, PACK, O], F32, "top")
+        a_rows = []
         for t in range(PACK):
-            if t < 2:
+            if t < 4:
                 nc.scalar.activation(out=b4[:, t, :], in_=b_rows[t][:].indirect(list4[:]), func=COPY)
             else:
                 nc.vector.tensor_copy(out=b4[:, t, :], in_=b_rows[t][:].indirect(list4[:]))
         for t in range(PACK):
             nc.vector.tensor_copy(out=b3[:, t, :], in_=b_rows[t][:].indirect(list3[:]))
+        for t in range(PACK):
+            a_rows.append(tile([P, J], F32, "a_row%d" % t, tag=None if t < 2 else "b_row%d" % t))
+            if t < 2:
+                nc.scalar.copy(out=a_rows[t][:], in_=a_acc[t][:])
+            else:
+                nc.vector.tensor_copy(out=a_rows[t][:], in_=a_acc[t][:])
             nc.scalar.activation(
                 out=sig[:, t, :], in_=a_rows[t][:].indirect(list4[:]), func=SIGMOID,
                 scale=sg_t[:, t : t + 1],
             )
-        gate = sb.tile([P, HALVES, O], F32, name="gate", tag="a_row3", align_bytes=64)
+        gate = tile([P, HALVES, O], F32, "gate", tag="b_row3")
         for h in range(HALVES):
             nc.scalar.activation(
                 out=gate[:, h, :], in_=tz_t[h][:].indirect(list5[:]), func=SIGMOID,
                 bias=bo_t[:, h : h + 1], scale=so_t[:, h : h + 1],
             )
-
         nc.vector.tensor_tensor(out=top[:], in0=b3[:], in1=b4[:], op=MAX)
         hid = tile([P, O, PACK], BF16, "hid")
         nc.vector.tensor_tensor(

@@ -21,16 +21,11 @@ MAX = mybir.AluOpType.max
 
 P = 128
 PACK = 4
-QUADS = 4
+GROUP = 16
 HALVES = N // P
-
-
-def load_scales(queue, plane, scales, quads):
-    for q in quads:
-        queue.dma_start(
-            out=plane[32 * q : 32 * q + 4, :].bitcast(I32),
-            in_=scales[0, 4 * q : 4 * q + 4, :].bitcast(I32),
-        )
+RUN = 4
+LOW_QUADS, HIGH_QUADS, ALL_QUADS = (0, 1), (2, 3), (0, 1, 2, 3)
+A_SLICES_ON_SCALAR = 2
 
 
 def tile_list_twotab_agree_one_finalgate_kernel(
@@ -45,185 +40,180 @@ def tile_list_twotab_agree_one_finalgate_kernel(
         def tile(shape, dtype, name, tag=None):
             return sb.tile(shape, dtype, name=name, tag=tag or name, align_bytes=64)
 
-        list1 = tile([P, J // 16], U16, "list1")
-        list2 = tile([P, J // 16], U16, "list2")
-        list3 = tile([P, O // 16], U16, "list3")
-        list4 = tile([P, O // 16], U16, "list4")
-        list5 = tile([P, O // 16], U16, "list5")
-        xo_w = tile([P, Z], I32, "xo_w")
-        xt_w = tile([P, T], I32, "xt_w")
-        xo_s = tile([P, Z], U8, "xo_s")
-        xt_s = tile([P, T], U8, "xt_s")
-        w2_raw = tile([P, 2 * R], U8, "w2_raw")
-        w_raw = tile([P, 2 * R], U8, "w_raw")
-        w2_sraw = tile([P, R], U8, "w2_sraw")
-        w_sraw = tile([P, R], U8, "w_sraw")
-        wb_w = tile([P, 2 * N], U8, "wb_w")
-        wb_s = tile([P, N], U8, "wb_s")
-        sg_t = tile([P, PACK], F32, "sg_t")
-        so_t = tile([P, HALVES], F32, "so_t")
-        bo_t = tile([P, HALVES], F32, "bo_t")
-        tz_t = [tile([P, E], F32, "tz%d" % h) for h in range(HALVES)]
+        list1 = tile([P, J // GROUP], U16, "list1")
+        list2 = tile([P, J // GROUP], U16, "list2")
+        list3 = tile([P, O // GROUP], U16, "list3")
+        list4 = tile([P, O // GROUP], U16, "list4")
+        list5 = tile([P, O // GROUP], U16, "list5")
+        xo_table = tile([P, Z], I32, "xo_table")
+        xt_table = tile([P, T], I32, "xt_table")
+        xo_plane = tile([P, Z], U8, "xo_plane")
+        xt_plane = tile([P, T], U8, "xt_plane")
+        w2_loaded = tile([P, 2 * R], U8, "w2_loaded")
+        w_loaded = tile([P, 2 * R], U8, "w_loaded")
+        w2_plane = tile([P, R], U8, "w2_plane")
+        w_plane = tile([P, R], U8, "w_plane")
+        wb_loaded = tile([P, 2 * N], U8, "wb_loaded")
+        wb_plane = tile([P, N], U8, "wb_plane")
+        sg_cols = tile([P, PACK], F32, "sg_cols")
+        so_cols = tile([P, HALVES], F32, "so_cols")
+        bo_cols = tile([P, HALVES], F32, "bo_cols")
+        tz_rows = [tile([P, E], F32, "tz_rows%d" % h) for h in range(HALVES)]
 
-        def clear_odd(plane):
-            words = plane[:].bitcast(I32)
-            cut = words.shape[1] // 2 + 1
-            nc.vector.memset(words[:, :cut], 0)
-            nc.vector.memset(words[:, cut:], 0)
+        def load_plane(queue, plane, scales, quads):
+            for q in quads:
+                queue.dma_start(
+                    out=plane[32 * q : 32 * q + 4, :].bitcast(I32),
+                    in_=scales[0, 4 * q : 4 * q + 4, :].bitcast(I32),
+                )
 
-        def load_table(queue, dst, words):
-            queue.dma_start(out=dst[:], in_=words[0].rearrange("p n t -> p (n t)").bitcast(I32))
+        def load_table(queue, table, words):
+            queue.dma_start(out=table[:], in_=words[0].rearrange("p n t -> p (n t)").bitcast(I32))
 
-        def load_raw(queue, dst, words):
-            queue.dma_start(out=dst[:].bitcast(I32), in_=words[0].bitcast(I32))
+        def load_weight(queue, loaded, words):
+            queue.dma_start(out=loaded[:].bitcast(I32), in_=words[0].bitcast(I32))
 
-        def load_cols(queue, dst, vec):
+        def load_halves(cols, vector):
             with nc.allow_non_contiguous_dma(reason="one value a partition and half"):
-                queue.dma_start(out=dst[:], in_=vec.rearrange("(h p) one -> p (h one)", p=P))
+                nc.sync.dma_start(out=cols[:], in_=vector.rearrange("(h p) one -> p (h one)", p=P))
 
-        def load_sg(queue):
-            queue.dma_start(out=sg_t[:], in_=sg.rearrange("(p t) one -> p (t one)", t=PACK))
+        nc.vector.memset(w2_plane[:].bitcast(I32), 0)
+        nc.vector.memset(w_plane[:].bitcast(I32), 0)
+        for plane in (xo_plane, xt_plane, wb_plane):
+            plane_words = plane[:].bitcast(I32)
+            cut = plane_words.shape[1] // 2 + 1
+            nc.vector.memset(plane_words[:, :cut], 0)
+            nc.vector.memset(plane_words[:, cut:], 0)
 
-        def load_tz(queue, h):
-            queue.dma_start(out=tz_t[h][:], in_=tz[h * P : (h + 1) * P, :])
+        load_plane(nc.gpsimd, w_plane, w_scales, HIGH_QUADS)
+        load_plane(nc.gpsimd, wb_plane, wb_scales, ALL_QUADS[1:])
 
-        def warm_up():
-            warm = tile([P, 2], F32, "warm")
-            nc.vector.memset(warm[:, 0:1], 0.0)
-            nc.scalar.activation(out=warm[:, 1:2], in_=warm[:, 0:1], func=SIGMOID)
+        load_weight(nc.scalar, w2_loaded, w2_words)
+        load_plane(nc.scalar, w2_plane, w2_scales, HIGH_QUADS)
+        load_table(nc.scalar, xo_table, xo_words)
+        load_plane(nc.scalar, xo_plane, xo_scales, HIGH_QUADS)
 
-        nc.vector.memset(w2_sraw[:].bitcast(I32), 0)
-        nc.vector.memset(w_sraw[:].bitcast(I32), 0)
-        for plane in (xo_s, xt_s, wb_s):
-            clear_odd(plane)
-        load_scales(nc.gpsimd, w_sraw, w_scales, range(2, 4))
-        load_scales(nc.gpsimd, wb_s, wb_scales, range(QUADS))
-        load_raw(nc.scalar, w2_raw, w2_words)
-        load_scales(nc.scalar, w2_sraw, w2_scales, range(2, 4))
-        load_table(nc.scalar, xo_w, xo_words)
-        warm_up()
+        warm = tile([P, 2], F32, "warm")
+        nc.vector.memset(warm[:, 0:1], 0.0)
+        nc.scalar.activation(out=warm[:, 1:2], in_=warm[:, 0:1], func=SIGMOID)
+
         nc.sync.dma_start(list2[:], offs2)
-        load_raw(nc.sync, w_raw, w_words)
-        load_scales(nc.sync, w2_sraw, w2_scales, range(2))
-        load_scales(nc.sync, xo_s, xo_scales, range(QUADS))
-        load_scales(nc.sync, w_sraw, w_scales, range(2))
-        load_table(nc.sync, xt_w, xt_words)
+        load_weight(nc.sync, w_loaded, w_words)
+        load_plane(nc.sync, w2_plane, w2_scales, LOW_QUADS)
+        load_plane(nc.sync, xo_plane, xo_scales, LOW_QUADS)
+        load_plane(nc.sync, w_plane, w_scales, LOW_QUADS)
+        load_table(nc.sync, xt_table, xt_words)
         nc.sync.dma_start(list1[:], offs)
-        load_scales(nc.sync, xt_s, xt_scales, range(QUADS))
+        load_plane(nc.sync, xt_plane, xt_scales, ALL_QUADS)
         nc.sync.dma_start(list4[:], offs4)
         nc.sync.dma_start(list3[:], offs3)
-        load_sg(nc.sync)
+        nc.sync.dma_start(out=sg_cols[:], in_=sg.rearrange("(p t) one -> p (t one)", t=PACK))
         nc.sync.dma_start(list5[:], offs5)
-        load_cols(nc.sync, so_t, so)
-        load_cols(nc.sync, bo_t, bo)
-        load_tz(nc.sync, 0)
-        load_tz(nc.sync, 1)
-        load_raw(nc.sync, wb_w, wb_words)
+        load_halves(so_cols, so)
+        load_halves(bo_cols, bo)
+        for h in range(HALVES):
+            nc.sync.dma_start(out=tz_rows[h][:], in_=tz[h * P : (h + 1) * P, :])
+        load_weight(nc.sync, wb_loaded, wb_words)
+        load_plane(nc.sync, wb_plane, wb_scales, ALL_QUADS[:1])
 
-        def deal_words(name, raw):
-            wd = tile([P, 2 * R], U8, name)
-            nc.scalar.copy(
-                out=wd[:].bitcast(U16).rearrange("p (t m) -> p t m", t=PACK),
-                in_=raw[:].bitcast(U16).rearrange("p (m t) -> p t m", t=PACK),
-            )
-            return wd
-
-        def deal_scales(name, sraw):
-            ws = tile([P, R], U8, name)
+        def deal(dealt, loaded):
             nc.vector.tensor_copy(
-                out=ws[:].rearrange("p (t m) -> p t m", t=PACK),
-                in_=sraw[:].rearrange("p (m t) -> p t m", t=PACK),
+                out=dealt.rearrange("p (t m) -> p t m", t=PACK), in_=loaded.rearrange("p (m t) -> p t m", t=PACK)
             )
-            return ws
 
-        def products(name, wd, ws, gw, gs, fmt):
-            accs = []
+        def first_stage(name, dealt_words, dealt_plane, picked_words, picked_plane, fmt):
+            sums = []
             for t in range(PACK):
-                acc = ps.tile([P, J], F32, name="%s_acc%d" % (name, t), tag="%s_bank%d" % (name, t))
+                bank = ps.tile([P, J], F32, name="%s_sum%d" % (name, t), tag="%s_bank%d" % (name, t))
                 nc.tensor.matmul_mx(
-                    out=acc[:],
-                    lhsT=wd[:, 2 * P * t : 2 * P * (t + 1)].bitcast(E2M1),
-                    lhsT_scale=ws[:, P * t : P * (t + 1)],
-                    rhs=gw[:].bitcast(fmt),
-                    rhs_scale=gs[:],
+                    out=bank[:],
+                    lhsT=dealt_words[:, 2 * P * t : 2 * P * (t + 1)].bitcast(E2M1),
+                    lhsT_scale=dealt_plane[:, P * t : P * (t + 1)],
+                    rhs=picked_words[:].bitcast(fmt),
+                    rhs_scale=picked_plane[:],
                     start=True,
                     stop=True,
                 )
-                accs.append(acc)
-            return accs
+                sums.append(bank)
+            return sums
 
-        w2_d = deal_words("w2_d", w2_raw)
-        w_d = deal_words("w_d", w_raw)
+        w2_dealt = tile([P, 2 * R], U8, "w2_dealt")
+        w_dealt = tile([P, 2 * R], U8, "w_dealt")
+        deal(w2_dealt[:].bitcast(U16), w2_loaded[:].bitcast(U16))
+        deal(w_dealt[:].bitcast(U16), w_loaded[:].bitcast(U16))
 
-        w2_ds = deal_scales("w2_ds", w2_sraw)
-        xo_gw = tile([P, J], U32, "xo_gw")
-        xo_gs = tile([P, J], U8, "xo_gs")
-        nc.vector.tensor_copy(out=xo_gw[:], in_=xo_w[:].bitcast(U32).indirect(list2[:]))
-        nc.vector.tensor_copy(out=xo_gs[:], in_=xo_s[:].indirect(list2[:]))
-        b_acc = products("b", w2_d, w2_ds, xo_gw, xo_gs, E4M3)
-        b_rows = [tile([P, J], F32, "b_row%d" % t) for t in range(PACK)]
+        w2_dealt_plane = tile([P, R], U8, "w2_dealt_plane")
+        deal(w2_dealt_plane[:], w2_plane[:])
+        xo_picked = tile([P, J], U32, "xo_picked")
+        xo_picked_plane = tile([P, J], U8, "xo_picked_plane")
+        nc.vector.tensor_copy(out=xo_picked[:], in_=xo_table[:].bitcast(U32).indirect(list2[:]))
+        nc.vector.tensor_copy(out=xo_picked_plane[:], in_=xo_plane[:].indirect(list2[:]))
+        b_sums = first_stage("b", w2_dealt, w2_dealt_plane, xo_picked, xo_picked_plane, E4M3)
+        b_rows = [tile([P, J], F32, "b_rows%d" % t) for t in range(PACK)]
         for t in range(PACK):
-            nc.scalar.copy(out=b_rows[t][:], in_=b_acc[t][:])
+            nc.scalar.copy(out=b_rows[t][:], in_=b_sums[t][:])
 
-        w_ds = deal_scales("w_ds", w_sraw)
-        xt_gw = tile([P, J], U32, "xt_gw", tag="w_sraw")
-        xt_gs = tile([P, J], U8, "xt_gs")
-        nc.vector.tensor_copy(out=xt_gw[:], in_=xt_w[:].bitcast(U32).indirect(list1[:]))
-        nc.vector.tensor_copy(out=xt_gs[:], in_=xt_s[:].indirect(list1[:]))
-        a_acc = products("a", w_d, w_ds, xt_gw, xt_gs, E5M2)
+        w_dealt_plane = tile([P, R], U8, "w_dealt_plane")
+        deal(w_dealt_plane[:], w_plane[:])
+        xt_picked = tile([P, J], U32, "xt_picked", tag="w_plane")
+        xt_picked_plane = tile([P, J], U8, "xt_picked_plane")
+        nc.vector.tensor_copy(out=xt_picked[:], in_=xt_table[:].bitcast(U32).indirect(list1[:]))
+        nc.vector.tensor_copy(out=xt_picked_plane[:], in_=xt_plane[:].indirect(list1[:]))
+        a_sums = first_stage("a", w_dealt, w_dealt_plane, xt_picked, xt_picked_plane, E5M2)
 
-        b3 = tile([P, PACK, O], F32, "b3")
-        b4 = tile([P, PACK, O], F32, "b4")
-        sig = tile([P, PACK, O], F32, "sig")
-        top = tile([P, PACK, O], F32, "top")
-        a_rows = []
+        b_at3 = tile([P, PACK, O], F32, "b_at3")
+        b_at4 = tile([P, PACK, O], F32, "b_at4")
+        hid_gate = tile([P, PACK, O], F32, "hid_gate")
+        larger = tile([P, PACK, O], F32, "larger")
         for t in range(PACK):
-            if t < 4:
-                nc.scalar.activation(out=b4[:, t, :], in_=b_rows[t][:].indirect(list4[:]), func=COPY)
+            nc.scalar.activation(out=b_at4[:, t, :], in_=b_rows[t][:].indirect(list4[:]), func=COPY)
+        for t in range(PACK):
+            nc.vector.tensor_copy(out=b_at3[:, t, :], in_=b_rows[t][:].indirect(list3[:]))
+
+        for t in range(PACK):
+            if t < A_SLICES_ON_SCALAR:
+                a_rows = tile([P, J], F32, "a_rows%d" % t)
+                nc.scalar.copy(out=a_rows[:], in_=a_sums[t][:])
             else:
-                nc.vector.tensor_copy(out=b4[:, t, :], in_=b_rows[t][:].indirect(list4[:]))
-        for t in range(PACK):
-            nc.vector.tensor_copy(out=b3[:, t, :], in_=b_rows[t][:].indirect(list3[:]))
-        for t in range(PACK):
-            a_rows.append(tile([P, J], F32, "a_row%d" % t, tag=None if t < 2 else "b_row%d" % t))
-            if t < 2:
-                nc.scalar.copy(out=a_rows[t][:], in_=a_acc[t][:])
-            else:
-                nc.vector.tensor_copy(out=a_rows[t][:], in_=a_acc[t][:])
+                a_rows = tile([P, J], F32, "a_rows%d" % t, tag="b_rows%d" % t)
+                nc.vector.tensor_copy(out=a_rows[:], in_=a_sums[t][:])
             nc.scalar.activation(
-                out=sig[:, t, :], in_=a_rows[t][:].indirect(list4[:]), func=SIGMOID,
-                scale=sg_t[:, t : t + 1],
+                out=hid_gate[:, t, :], in_=a_rows[:].indirect(list4[:]), func=SIGMOID, scale=sg_cols[:, t : t + 1]
             )
-        gate = tile([P, HALVES, O], F32, "gate", tag="b_row3")
+
+        out_gate = tile([P, HALVES, O], F32, "out_gate", tag="b_rows%d" % (PACK - 1))
         for h in range(HALVES):
             nc.scalar.activation(
-                out=gate[:, h, :], in_=tz_t[h][:].indirect(list5[:]), func=SIGMOID,
-                bias=bo_t[:, h : h + 1], scale=so_t[:, h : h + 1],
+                out=out_gate[:, h, :], in_=tz_rows[h][:].indirect(list5[:]), func=SIGMOID,
+                bias=bo_cols[:, h : h + 1], scale=so_cols[:, h : h + 1],
             )
-        nc.vector.tensor_tensor(out=top[:], in0=b3[:], in1=b4[:], op=MAX)
+
         hid = tile([P, O, PACK], BF16, "hid")
-        nc.vector.tensor_tensor(
-            out=hid[:].rearrange("p (c i) t -> p c t i", i=4),
-            in0=top[:].rearrange("p t (c i) -> p c t i", i=4),
-            in1=sig[:].rearrange("p t (c i) -> p c t i", i=4),
-            op=MULT,
-        )
-        hid_w = tile([P, O], U32, "hid_w")
-        hid_s = tile([P, O], U8, "hid_s")
+        for pair in (slice(0, PACK // 2), slice(PACK // 2, PACK)):
+            nc.vector.tensor_tensor(out=larger[:, pair, :], in0=b_at3[:, pair, :], in1=b_at4[:, pair, :], op=MAX)
+            nc.vector.tensor_tensor(
+                out=hid[:, :, pair].rearrange("p (c i) t -> p c t i", i=RUN),
+                in0=larger[:, pair, :].rearrange("p t (c i) -> p c t i", i=RUN),
+                in1=hid_gate[:, pair, :].rearrange("p t (c i) -> p c t i", i=RUN),
+                op=MULT,
+            )
+        hid_words = tile([P, O], U32, "hid_words")
+        hid_plane = tile([P, O], U8, "hid_plane")
         nc.vector.quantize_mx(
-            out=hid_w[:].bitcast(E4M3), scales=hid_s[:], in_=hid[:].rearrange("p o t -> p (o t)")
+            out=hid_words[:].bitcast(E4M3), scales=hid_plane[:], in_=hid[:].rearrange("p o t -> p (o t)")
         )
+
         for h, queue in enumerate((nc.sync, nc.scalar)):
-            pacc = ps.tile([P, O], F32, name="pacc%d" % h, tag="b_bank%d" % h)
+            p_sum = ps.tile([P, O], F32, name="p_sum%d" % h, tag="b_bank%d" % h)
             nc.tensor.matmul_mx(
-                out=pacc[:],
-                lhsT=wb_w[:, 2 * P * h : 2 * P * (h + 1)].bitcast(E2M1),
-                lhsT_scale=wb_s[:, P * h : P * (h + 1)],
-                rhs=hid_w[:].bitcast(E4M3),
-                rhs_scale=hid_s[:],
+                out=p_sum[:],
+                lhsT=wb_loaded[:, 2 * P * h : 2 * P * (h + 1)].bitcast(E2M1),
+                lhsT_scale=wb_plane[:, P * h : P * (h + 1)],
+                rhs=hid_words[:].bitcast(E4M3),
+                rhs_scale=hid_plane[:],
                 start=True,
                 stop=True,
             )
-            res = tile([P, O], F32, "res%d" % h)
-            nc.vector.tensor_tensor(out=res[:], in0=pacc[:], in1=gate[:, h, :], op=MULT)
-            queue.dma_start(out=out[h * P : (h + 1) * P, :], in_=res[:])
+            result = tile([P, O], F32, "result%d" % h)
+            nc.vector.tensor_tensor(out=result[:], in0=p_sum[:], in1=out_gate[:, h, :], op=MULT)
+            queue.dma_start(out=out[h * P : (h + 1) * P, :], in_=result[:])

from contextlib import ExitStack

import concourse.mybir as mybir

K, F, T, Z, J, R, O, N, E = 512, 512, 1024, 1024, 256, 512, 128, 256, 512
FLOPS = 2 * K * R * J + 2 * F * R * J + 2 * R * N * O

F32 = mybir.dt.float32
BF16 = mybir.dt.bfloat16
I32 = mybir.dt.int32
U32 = mybir.dt.uint32
U16 = mybir.dt.uint16
U8 = mybir.dt.uint8
E4M3 = mybir.dt.float8_e4m3fn_x4
E5M2 = mybir.dt.float8_e5m2_x4
E2M1 = mybir.dt.float4_e2m1fn_x4
SIGMOID = mybir.ActivationFunctionType.Sigmoid
COPY = mybir.ActivationFunctionType.Copy
MULT = mybir.AluOpType.mult
MAX = mybir.AluOpType.max

P = 128
PACK = 4
GROUP = 16
HALVES = N // P
RUN = 4
LOW_QUADS, HIGH_QUADS, ALL_QUADS = (0, 1), (2, 3), (0, 1, 2, 3)
A_SLICES_ON_SCALAR = 2


def tile_list_twotab_agree_one_finalgate_kernel(
    tc, xt_words, xt_scales, w_words, w_scales, xo_words, xo_scales, w2_words, w2_scales,
    sg, wb_words, wb_scales, tz, so, bo, offs, offs2, offs3, offs4, offs5, out,
):
    nc = tc.nc
    with ExitStack() as ctx:
        sb = ctx.enter_context(tc.tile_pool(name="sb", bufs=1))
        ps = ctx.enter_context(tc.psum_pool(name="ps", bufs=1))

        def tile(shape, dtype, name, tag=None):
            return sb.tile(shape, dtype, name=name, tag=tag or name, align_bytes=64)

        list1 = tile([P, J // GROUP], U16, "list1")
        list2 = tile([P, J // GROUP], U16, "list2")
        list3 = tile([P, O // GROUP], U16, "list3")
        list4 = tile([P, O // GROUP], U16, "list4")
        list5 = tile([P, O // GROUP], U16, "list5")
        xo_table = tile([P, Z], I32, "xo_table")
        xt_table = tile([P, T], I32, "xt_table")
        xo_plane = tile([P, Z], U8, "xo_plane")
        xt_plane = tile([P, T], U8, "xt_plane")
        w2_loaded = tile([P, 2 * R], U8, "w2_loaded")
        w_loaded = tile([P, 2 * R], U8, "w_loaded")
        w2_plane = tile([P, R], U8, "w2_plane")
        w_plane = tile([P, R], U8, "w_plane")
        wb_loaded = tile([P, 2 * N], U8, "wb_loaded")
        wb_plane = tile([P, N], U8, "wb_plane")
        sg_cols = tile([P, PACK], F32, "sg_cols")
        so_cols = tile([P, HALVES], F32, "so_cols")
        bo_cols = tile([P, HALVES], F32, "bo_cols")
        tz_rows = [tile([P, E], F32, "tz_rows%d" % h) for h in range(HALVES)]

        def load_plane(queue, plane, scales, quads):
            for q in quads:
                queue.dma_start(
                    out=plane[32 * q : 32 * q + 4, :].bitcast(I32),
                    in_=scales[0, 4 * q : 4 * q + 4, :].bitcast(I32),
                )

        def load_table(queue, table, words):
            queue.dma_start(out=table[:], in_=words[0].rearrange("p n t -> p (n t)").bitcast(I32))

        def load_weight(queue, loaded, words):
            queue.dma_start(out=loaded[:].bitcast(I32), in_=words[0].bitcast(I32))

        def load_halves(cols, vector):
            with nc.allow_non_contiguous_dma(reason="one value a partition and half"):
                nc.sync.dma_start(out=cols[:], in_=vector.rearrange("(h p) one -> p (h one)", p=P))

        nc.vector.memset(w2_plane[:].bitcast(I32), 0)
        nc.vector.memset(w_plane[:].bitcast(I32), 0)
        for plane in (xo_plane, xt_plane, wb_plane):
            plane_words = plane[:].bitcast(I32)
            cut = plane_words.shape[1] // 2 + 1
            nc.vector.memset(plane_words[:, :cut], 0)
            nc.vector.memset(plane_words[:, cut:], 0)

        load_plane(nc.gpsimd, w_plane, w_scales, HIGH_QUADS)
        load_plane(nc.gpsimd, wb_plane, wb_scales, ALL_QUADS[1:])

        load_weight(nc.scalar, w2_loaded, w2_words)
        load_plane(nc.scalar, w2_plane, w2_scales, HIGH_QUADS)
        load_table(nc.scalar, xo_table, xo_words)
        load_plane(nc.scalar, xo_plane, xo_scales, HIGH_QUADS)

        warm = tile([P, 2], F32, "warm")
        nc.vector.memset(warm[:, 0:1], 0.0)
        nc.scalar.activation(out=warm[:, 1:2], in_=warm[:, 0:1], func=SIGMOID)

        nc.sync.dma_start(list2[:], offs2)
        load_weight(nc.sync, w_loaded, w_words)
        load_plane(nc.sync, w2_plane, w2_scales, LOW_QUADS)
        load_plane(nc.sync, xo_plane, xo_scales, LOW_QUADS)
        load_plane(nc.sync, w_plane, w_scales, LOW_QUADS)
        load_table(nc.sync, xt_table, xt_words)
        nc.sync.dma_start(list1[:], offs)
        load_plane(nc.sync, xt_plane, xt_scales, ALL_QUADS)
        nc.sync.dma_start(list4[:], offs4)
        nc.sync.dma_start(list3[:], offs3)
        nc.sync.dma_start(out=sg_cols[:], in_=sg.rearrange("(p t) one -> p (t one)", t=PACK))
        nc.sync.dma_start(list5[:], offs5)
        load_halves(so_cols, so)
        load_halves(bo_cols, bo)
        for h in range(HALVES):
            nc.sync.dma_start(out=tz_rows[h][:], in_=tz[h * P : (h + 1) * P, :])
        load_weight(nc.sync, wb_loaded, wb_words)
        load_plane(nc.sync, wb_plane, wb_scales, ALL_QUADS[:1])

        def deal(dealt, loaded):
            nc.vector.tensor_copy(
                out=dealt.rearrange("p (t m) -> p t m", t=PACK), in_=loaded.rearrange("p (m t) -> p t m", t=PACK)
            )

        def first_stage(name, dealt_words, dealt_plane, picked_words, picked_plane, fmt):
            sums = []
            for t in range(PACK):
                bank = ps.tile([P, J], F32, name="%s_sum%d" % (name, t), tag="%s_bank%d" % (name, t))
                nc.tensor.matmul_mx(
                    out=bank[:],
                    lhsT=dealt_words[:, 2 * P * t : 2 * P * (t + 1)].bitcast(E2M1),
                    lhsT_scale=dealt_plane[:, P * t : P * (t + 1)],
                    rhs=picked_words[:].bitcast(fmt),
                    rhs_scale=picked_plane[:],
                    start=True,
                    stop=True,
                )
                sums.append(bank)
            return sums

        w2_dealt = tile([P, 2 * R], U8, "w2_dealt")
        w_dealt = tile([P, 2 * R], U8, "w_dealt")
        deal(w2_dealt[:].bitcast(U16), w2_loaded[:].bitcast(U16))
        deal(w_dealt[:].bitcast(U16), w_loaded[:].bitcast(U16))

        w2_dealt_plane = tile([P, R], U8, "w2_dealt_plane")
        deal(w2_dealt_plane[:], w2_plane[:])
        xo_picked = tile([P, J], U32, "xo_picked")
        xo_picked_plane = tile([P, J], U8, "xo_picked_plane")
        nc.vector.tensor_copy(out=xo_picked[:], in_=xo_table[:].bitcast(U32).indirect(list2[:]))
        nc.vector.tensor_copy(out=xo_picked_plane[:], in_=xo_plane[:].indirect(list2[:]))
        b_sums = first_stage("b", w2_dealt, w2_dealt_plane, xo_picked, xo_picked_plane, E4M3)
        b_rows = [tile([P, J], F32, "b_rows%d" % t) for t in range(PACK)]
        for t in range(PACK):
            nc.scalar.copy(out=b_rows[t][:], in_=b_sums[t][:])

        w_dealt_plane = tile([P, R], U8, "w_dealt_plane")
        deal(w_dealt_plane[:], w_plane[:])
        xt_picked = tile([P, J], U32, "xt_picked", tag="w_plane")
        xt_picked_plane = tile([P, J], U8, "xt_picked_plane")
        nc.vector.tensor_copy(out=xt_picked[:], in_=xt_table[:].bitcast(U32).indirect(list1[:]))
        nc.vector.tensor_copy(out=xt_picked_plane[:], in_=xt_plane[:].indirect(list1[:]))
        a_sums = first_stage("a", w_dealt, w_dealt_plane, xt_picked, xt_picked_plane, E5M2)

        b_at3 = tile([P, PACK, O], F32, "b_at3")
        b_at4 = tile([P, PACK, O], F32, "b_at4")
        hid_gate = tile([P, PACK, O], F32, "hid_gate")
        larger = tile([P, PACK, O], F32, "larger")
        for t in range(PACK):
            nc.scalar.activation(out=b_at4[:, t, :], in_=b_rows[t][:].indirect(list4[:]), func=COPY)
        for t in range(PACK):
            nc.vector.tensor_copy(out=b_at3[:, t, :], in_=b_rows[t][:].indirect(list3[:]))

        for t in range(PACK):
            if t < A_SLICES_ON_SCALAR:
                a_rows = tile([P, J], F32, "a_rows%d" % t)
                nc.scalar.copy(out=a_rows[:], in_=a_sums[t][:])
            else:
                a_rows = tile([P, J], F32, "a_rows%d" % t, tag="b_rows%d" % t)
                nc.vector.tensor_copy(out=a_rows[:], in_=a_sums[t][:])
            nc.scalar.activation(
                out=hid_gate[:, t, :], in_=a_rows[:].indirect(list4[:]), func=SIGMOID, scale=sg_cols[:, t : t + 1]
            )

        out_gate = tile([P, HALVES, O], F32, "out_gate", tag="b_rows%d" % (PACK - 1))
        for h in range(HALVES):
            nc.scalar.activation(
                out=out_gate[:, h, :], in_=tz_rows[h][:].indirect(list5[:]), func=SIGMOID,
                bias=bo_cols[:, h : h + 1], scale=so_cols[:, h : h + 1],
            )

        hid = tile([P, O, PACK], BF16, "hid")
        for pair in (slice(0, PACK // 2), slice(PACK // 2, PACK)):
            nc.vector.tensor_tensor(out=larger[:, pair, :], in0=b_at3[:, pair, :], in1=b_at4[:, pair, :], op=MAX)
            nc.vector.tensor_tensor(
                out=hid[:, :, pair].rearrange("p (c i) t -> p c t i", i=RUN),
                in0=larger[:, pair, :].rearrange("p t (c i) -> p c t i", i=RUN),
                in1=hid_gate[:, pair, :].rearrange("p t (c i) -> p c t i", i=RUN),
                op=MULT,
            )
        hid_words = tile([P, O], U32, "hid_words")
        hid_plane = tile([P, O], U8, "hid_plane")
        nc.vector.quantize_mx(
            out=hid_words[:].bitcast(E4M3), scales=hid_plane[:], in_=hid[:].rearrange("p o t -> p (o t)")
        )

        for h, queue in enumerate((nc.sync, nc.scalar)):
            p_sum = ps.tile([P, O], F32, name="p_sum%d" % h, tag="b_bank%d" % h)
            nc.tensor.matmul_mx(
                out=p_sum[:],
                lhsT=wb_loaded[:, 2 * P * h : 2 * P * (h + 1)].bitcast(E2M1),
                lhsT_scale=wb_plane[:, P * h : P * (h + 1)],
                rhs=hid_words[:].bitcast(E4M3),
                rhs_scale=hid_plane[:],
                start=True,
                stop=True,
            )
            result = tile([P, O], F32, "result%d" % h)
            nc.vector.tensor_tensor(out=result[:], in0=p_sum[:], in1=out_gate[:, h, :], op=MULT)
            queue.dma_start(out=out[h * P : (h + 1) * P, :], in_=result[:])
